import numpy as np
import ml_dtypes


def mxq(x, axis, fmt="e4m3"):
    dtype, down = {"e4m3": (ml_dtypes.float8_e4m3fn, 7), "e5m2": (ml_dtypes.float8_e5m2, 14)}[fmt]
    v = np.moveaxis(np.asarray(x, np.float32).astype(ml_dtypes.bfloat16).astype(np.float64), axis, -1)
    blocks = v.reshape(v.shape[:-1] + (-1, 32))
    amax = np.abs(blocks).max(-1, keepdims=True)
    byte = np.maximum(np.where(amax > 0, np.frexp(amax)[1] - 1 + 127, 0) - down, 1)
    scale = np.exp2(byte - 127.0)
    codes = (blocks / scale).astype(np.float32).astype(dtype).astype(np.float64)
    return np.moveaxis((codes * scale).reshape(v.shape), -1, axis)


WIDE = False


def mx_kscale(k, group=512):
    if not WIDE:
        return np.ones(k)
    levels = np.array([18, -18])
    if group != 512:
        return np.exp2(np.random.permutation(np.resize(levels, k // group))).repeat(group)
    if k % 512:
        return np.exp2(np.random.permutation(np.resize(levels, k // 32))).repeat(32)
    a = np.empty((k // 512, 16))
    for p in range(k // 512):
        a[p, :8] = np.random.permutation(np.resize(levels, 8))
        for g in range(8):
            far = levels[np.abs(levels - a[p, g]) >= 10]
            a[p, g + 8] = far[np.random.randint(len(far))]
    return np.exp2(a.ravel()).repeat(32)


def f64(x):
    return np.asarray(x).astype(np.float64)


K, R, M, N = 1024, 128, 512, 512


def setup_inputs():
    n = np.random.standard_normal
    s = mx_kscale(K)[:, None]
    z = mx_kscale(R, 0)
    return {
        "x": (n((K, N)) * s).astype(np.float32),
        "w": (n((K, M)) / np.sqrt(K) / s).astype(np.float32),
        "a": (n((K, R)) / np.sqrt(K) / s * z).astype(np.float32),
        "bb": (n((R, M)) / np.sqrt(R) / z[:, None]).astype(np.float32),
    }


def reference(x, w, a, bb):
    xq = mxq(f64(x), 0, "e4m3")
    z = mxq(f64(a), 0, "e4m3").T @ xq
    y = (mxq(f64(w), 0, "e4m3").T @ xq) + (mxq(f64(bb), 0, "e4m3").T @ mxq(z, 0, "e4m3"))
    return y

@@ -1,0 +1,206 @@
+from contextlib import ExitStack
+
+import concourse.mybir as mybir
+
+K, R, M, N = 1024, 128, 512, 512
+FLOPS = 2 * K * N * (M + R) + 2 * R * M * N
+
+F32 = mybir.dt.float32
+BF16 = mybir.dt.bfloat16
+I32 = mybir.dt.int32
+U32 = mybir.dt.uint32
+U8 = mybir.dt.uint8
+FP8X4 = mybir.dt.float8_e4m3fn_x4
+
+P = 128
+PACK = 4
+K_PASS = P * PACK
+PASSES = K // K_PASS
+ROWS = R // PACK
+TILES = P // ROWS
+W = 128
+HALF = N // 2
+
+LOADS = "a0 a1 0.0 0.1 1.0 1.1 b 2.0 2.1 3.0 3.1 4.0 4.1 5.0 5.1 6.0 6.1 7.0 7.1"
+ORDER = "Vca0 Vca1 Vqa0 Vqa1 Sc00 Vra0 Sc01 Vq00 Vra1 Sc10 Vq01 Pzm0 Vc11 Vq10 Vq11 Vcb Szc0 Pzm1 Vc20 Vqb Vq20 Szc1 Vqz0 Vc21 Sc30 Plm0 Vqz1 Vq21 Plm1 Vh31a Sh31b Vq30 Pzm2 Slc10 Vc40 Slc00 Vq31 Vq40 Sc41 Vlc30 Pzm3 Vlc20 Szc2 Vq41 Sc50 Vc51 Pbm01 Pbm00 Vqz2 Szc3 Vq51 Vq50 Plm2 Sc60 Pbm11 Vqz3 Vad00 Plm3 Sc61 Vc70 Pbm10 Vq60 Sh71b Vq61 Vad10 Slc01 Pbm21 Vh71a Slc21 Vad01 Pbm20 Slc11 Vq70 Slc31 Vq71 Vad11 Pbm30 Vad21 Vad20 Pbm31 Vad30 Vad31"
+
+
+def tile_rows_lora_kernel(tc, x, w, a, bb, out):
+    nc = tc.nc
+
+    with ExitStack() as ctx:
+        sb = ctx.enter_context(tc.tile_pool(name="sb", bufs=1))
+        ps = ctx.enter_context(tc.psum_pool(name="ps", bufs=1))
+        ctx.enter_context(tc.manual_schedule())
+
+        whole = [ps.tile([P, N], F32, name=f"whole{i}") for i in range(4)]
+        lora = [ps.tile([P, N], F32, name=f"lora{g}") for g in range(TILES)]
+
+        def operand(name):
+            staged = sb.tile([P, W, PACK], BF16, name=name + "_bf", align_bytes=64)
+            codes = sb.tile([P, W], U32, name=name + "_codes", align_bytes=64)
+            scales = sb.tile([P, W], U8, name=name + "_scales", align_bytes=64)
+            return staged, codes, scales
+
+        def quantize(op):
+            staged, codes, scales = op
+            nc.vector.quantize_mx(
+                out=codes[:].bitcast(FP8X4),
+                scales=scales[:],
+                in_=staged[:].rearrange("p n t -> p (n t)"),
+            )
+
+        def gpsimd_copy(out, in_):
+            nc.gpsimd.tensor_scalar(out=out, in0=in_, scalar1=1.0, scalar2=0.0, op0=mybir.AluOpType.mult, op1=mybir.AluOpType.add)
+
+        def interleave(copy, op, raw, lo=0, hi=W):
+            copy(
+                out=op[0][:, lo:hi, :].rearrange("p (c i) t -> p c t i", i=4),
+                in_=raw[:, :, lo:hi].rearrange("p t (c i) -> p c t i", i=4),
+            )
+
+        warm = sb.tile([P, 8], F32, name="warm")
+        warm2 = sb.tile([P, 8], F32, name="warm2")
+        nc.vector.memset(warm[:], 0.0)
+        nc.scalar.copy(out=warm2[:], in_=warm[:])
+
+        raws = {}
+        for tok in LOADS.split():
+            if tok[0] == "a":
+                c = int(tok[1])
+                raw = sb.tile([P, PACK, R], F32, name=f"a_raw{c}")
+                nc.sync.dma_start(
+                    out=raw[:], in_=a[K_PASS * c : K_PASS * (c + 1), :].rearrange("(p t) r -> p t r", t=PACK)
+                )
+                raws[tok] = raw[:]
+            elif tok == "b":
+                raw = sb.tile([P, PACK, W], F32, name="bb_raw")
+                for g in (0, 2, 1, 3):
+                    nc.sync.dma_start(
+                        out=raw[ROWS * g : ROWS * (g + 1)],
+                        in_=bb[:, W * g : W * (g + 1)].rearrange("(p t) m -> p t m", t=PACK),
+                    )
+                raws[tok] = raw[:]
+            else:
+                parts = tok.split("+")
+                s, c = int(parts[0][0]), int(parts[0][2])
+                src = x if s < 4 else w
+                width = W * len(parts)
+                raw = sb.tile([P, PACK, width], F32, name=f"raw{s}_{c}")
+                nc.sync.dma_start(
+                    out=raw[:],
+                    in_=src[K_PASS * c : K_PASS * (c + 1), W * (s % 4) : W * (s % 4) + width].rearrange("(p t) n -> p t n", t=PACK),
+                )
+                for i in range(len(parts)):
+                    raws[f"{s + i}{c}"] = raw[:, :, W * i : W * (i + 1)]
+
+        ops = {key: operand("op" + key) for key in raws}
+        for c in range(PASSES):
+            nc.vector.memset(ops[f"a{c}"][2][:].bitcast(I32), 0)
+        a4_codes = [sb.tile([P, PACK, TILES, ROWS], I32, name=f"a4_codes{c}", align_bytes=64) for c in range(PASSES)]
+        a4_scales = [sb.tile([P, PACK, TILES, ROWS // 4], I32, name=f"a4_scales{c}", align_bytes=64) for c in range(PASSES)]
+        z_ops = [operand(f"z{i}") for i in range(4)]
+        lora_sb = [sb.tile([P, N], F32, name=f"lora_sb{g}") for g in range(TILES)]
+        result = [sb.tile([P, N], F32, name=f"result{g}") for g in range(TILES)]
+
+        def cast_a(copy, c):
+            copy(
+                out=ops[f"a{c}"][0][:].rearrange("p (j q) t -> p q j t", j=PACK),
+                in_=raws[f"a{c}"].rearrange("p t (q j) -> p q j t", j=PACK),
+            )
+
+        def replicate(c):
+            op = ops[f"a{c}"]
+            nc.vector.tensor_copy(
+                out=a4_codes[c][:],
+                in_=op[1][:].bitcast(I32).rearrange("p (u q) -> p u q", q=ROWS).unsqueeze(2).to_broadcast([P, PACK, TILES, ROWS]),
+            )
+            nc.vector.tensor_copy(
+                out=a4_scales[c][:],
+                in_=op[2][:].bitcast(I32).rearrange("p (u q) -> p u q", q=ROWS // 4).unsqueeze(2).to_broadcast([P, PACK, TILES, ROWS // 4]),
+            )
+
+        def z_matmuls(i):
+            for j in range(PACK):
+                for c in range(PASSES):
+                    nc.tensor.matmul_mx(
+                        out=whole[i][:, W * j : W * (j + 1)],
+                        lhsT=a4_codes[c][:, j].rearrange("p g q -> p (g q)").bitcast(FP8X4),
+                        lhsT_scale=a4_scales[c][:, j].rearrange("p g q -> p (g q)").bitcast(U8),
+                        rhs=ops[f"{i}{c}"][1][:].bitcast(FP8X4),
+                        rhs_scale=ops[f"{i}{c}"][2][:],
+                        start=(c == 0),
+                        stop=(c == PASSES - 1),
+                    )
+
+        def lora_matmuls(i):
+            for g in range(TILES):
+                rows = slice(ROWS * g, ROWS * (g + 1))
+                nc.tensor.matmul_mx(
+                    out=lora[g][:, W * i : W * (i + 1)],
+                    lhsT=ops["b"][1][rows, :].bitcast(FP8X4),
+                    lhsT_scale=ops["b"][2][rows, :],
+                    rhs=z_ops[i][1][rows, :].bitcast(FP8X4),
+                    rhs_scale=z_ops[i][2][rows, :],
+                    start=True,
+                    stop=True,
+                )
+
+        def base_bank(g, h):
+            return whole[0] if (g == 3 and h == 1) else whole[g]
+
+        def base_matmuls(g, h):
+            for i in (2 * h, 2 * h + 1):
+                for c in range(PASSES):
+                    nc.tensor.matmul_mx(
+                        out=base_bank(g, h)[:, W * i : W * (i + 1)],
+                        lhsT=ops[f"{4 + g}{c}"][1][:].bitcast(FP8X4),
+                        lhsT_scale=ops[f"{4 + g}{c}"][2][:],
+                        rhs=ops[f"{i}{c}"][1][:].bitcast(FP8X4),
+                        rhs_scale=ops[f"{i}{c}"][2][:],
+                        start=(c == 0),
+                        stop=(c == PASSES - 1),
+                    )
+
+        added = set()
+        stores = [((0, 0), (0, 1)), ((1, 0), (1, 1)), ((2, 0), (2, 1)), ((3, 0),), ((3, 1),)]
+        for tok in ORDER.split():
+            copy = {"V": nc.vector.tensor_copy, "S": nc.scalar.copy, "G": gpsimd_copy, "P": None}[tok[0]]
+            name = tok[1:]
+            if name.startswith("ca"):
+                cast_a(copy, int(name[2]))
+            elif name.startswith("ra"):
+                replicate(int(name[2]))
+            elif name.startswith("zm"):
+                z_matmuls(int(name[2]))
+            elif name.startswith("zc"):
+                i = int(name[2])
+                copy(out=z_ops[i][0][:], in_=whole[i][:].rearrange("p (j n) -> p n j", j=PACK))
+            elif name.startswith("qz"):
+                quantize(z_ops[int(name[2])])
+            elif name.startswith("lm"):
+                lora_matmuls(int(name[2]))
+            elif name.startswith("lc"):
+                g, h = int(name[2]), int(name[3])
+                cols = slice(HALF * h, HALF * (h + 1))
+                copy(out=lora_sb[g][:, cols], in_=lora[g][:, cols])
+            elif name.startswith("bm"):
+                base_matmuls(int(name[2]), int(name[3]))
+            elif name.startswith("ad"):
+                g, h = int(name[2]), int(name[3])
+                cols = slice(HALF * h, HALF * (h + 1))
+                nc.vector.tensor_add(out=result[g][:, cols], in0=base_bank(g, h)[:, cols], in1=lora_sb[g][:, cols])
+                added.add((g, h))
+                while stores and all(part in added for part in stores[0]):
+                    parts = stores.pop(0)
+                    g, lo, hi = parts[0][0], HALF * parts[0][1], HALF * (parts[-1][1] + 1)
+                    nc.sync.dma_start(out=out[W * g : W * (g + 1), lo:hi], in_=result[g][:, lo:hi])
+            elif name[0] == "c":
+                interleave(copy, ops[name[1:]], raws[name[1:]])
+            elif name[0] == "h":
+                lo = 0 if name[3] == "a" else W // 2
+                interleave(copy, ops[name[1:3]], raws[name[1:3]], lo, lo + W // 2)
+            elif name[0] == "q":
+                quantize(ops[name[1:]])
+            else:
+                raise ValueError(tok)

@@ -21,8 +21,8 @@ TILES = P // ROWS
 W = 128
 HALF = N // 2
 
-LOADS = "a0 a1 0.0 0.1 1.0 1.1 b 2.0 2.1 3.0 3.1 4.0 4.1 5.0 5.1 6.0 6.1 7.0 7.1"
-ORDER = "Vca0 Vca1 Vqa0 Vqa1 Sc00 Vra0 Sc01 Vq00 Vra1 Sc10 Vq01 Pzm0 Vc11 Vq10 Vq11 Vcb Szc0 Pzm1 Vc20 Vqb Vq20 Szc1 Vqz0 Vc21 Sc30 Plm0 Vqz1 Vq21 Plm1 Vh31a Sh31b Vq30 Pzm2 Slc10 Vc40 Slc00 Vq31 Vq40 Sc41 Vlc30 Pzm3 Vlc20 Szc2 Vq41 Sc50 Vc51 Pbm01 Pbm00 Vqz2 Szc3 Vq51 Vq50 Plm2 Sc60 Pbm11 Vqz3 Vad00 Plm3 Sc61 Vc70 Pbm10 Vq60 Sh71b Vq61 Vad10 Slc01 Pbm21 Vh71a Slc21 Vad01 Pbm20 Slc11 Vq70 Slc31 Vq71 Vad11 Pbm30 Vad21 Vad20 Pbm31 Vad30 Vad31"
+LOADS = "a0 a1 0.0+1.0+2.0+3.0 0.1+1.1 2.1+3.1 b 4.0+5.0+6.0+7.0 4.1+5.1 6.1 7.1"
+ORDER = "Vca0 Vqa0 Vca1 Vra0 Vqa1 Vra1 Vc00x2 Sc20x2 Vq00x2 Vq20x2 Vc01 Sc11 Vq01 Vq11 Pzm0 Pzm1 Vc21 Vh31a Sh31b Vq21 Vq31 Szc0 Pzm2 Vcb Szc1 Pzm3 Vqz0 Vqb Vzc2 Plm0 Vqz1 Szc3 Vqz2 Plm1 Plm2 Vc40 Sc60x2 Vqz3 Plm3 Vc50 Vq40x2 Slc0 Slc1 Vc41 Vc51 Vq41 Vq51 Pbm00 Pbm01 Pbm10 Pbm11 Vq60x2 Sc61 Vh71a Sh71b Vq61 Vq71 Pbm20 Pbm21 Slc2 Slc3 Vad0 Vad1 Pbm30 Pbm31 Vad2 Vad30 Vad31"
 
 
 def tile_rows_lora_kernel(tc, x, w, a, bb, out):
@@ -36,10 +36,10 @@ def tile_rows_lora_kernel(tc, x, w, a, bb, out):
         whole = [ps.tile([P, N], F32, name=f"whole{i}") for i in range(4)]
         lora = [ps.tile([P, N], F32, name=f"lora{g}") for g in range(TILES)]
 
-        def operand(name):
-            staged = sb.tile([P, W, PACK], BF16, name=name + "_bf", align_bytes=64)
-            codes = sb.tile([P, W], U32, name=name + "_codes", align_bytes=64)
-            scales = sb.tile([P, W], U8, name=name + "_scales", align_bytes=64)
+        def operand(name, width=W):
+            staged = sb.tile([P, width, PACK], BF16, name=name + "_bf", align_bytes=64)
+            codes = sb.tile([P, width], U32, name=name + "_codes", align_bytes=64)
+            scales = sb.tile([P, width], U8, name=name + "_scales", align_bytes=64)
             return staged, codes, scales
 
         def quantize(op):
@@ -49,6 +49,9 @@ def tile_rows_lora_kernel(tc, x, w, a, bb, out):
                 scales=scales[:],
                 in_=staged[:].rearrange("p n t -> p (n t)"),
             )
+
+        def window(op, lo, hi):
+            return op[0][:, lo:hi, :], op[1][:, lo:hi], op[2][:, lo:hi]
 
         def gpsimd_copy(out, in_):
             nc.gpsimd.tensor_scalar(out=out, in0=in_, scalar1=1.0, scalar2=0.0, op0=mybir.AluOpType.mult, op1=mybir.AluOpType.add)
@@ -70,7 +73,7 @@ def tile_rows_lora_kernel(tc, x, w, a, bb, out):
                 c = int(tok[1])
                 raw = sb.tile([P, PACK, R], F32, name=f"a_raw{c}")
                 nc.sync.dma_start(
-                    out=raw[:], in_=a[K_PASS * c : K_PASS * (c + 1), :].rearrange("(p t) r -> p t r", t=PACK)
+                    out=raw[:].rearrange("p t r -> p (t r)"), in_=a[K_PASS * c : K_PASS * (c + 1), :].rearrange("(p t) r -> p (t r)", t=PACK)
                 )
                 raws[tok] = raw[:]
             elif tok == "b":
@@ -87,14 +90,19 @@ def tile_rows_lora_kernel(tc, x, w, a, bb, out):
                 src = x if s < 4 else w
                 width = W * len(parts)
                 raw = sb.tile([P, PACK, width], F32, name=f"raw{s}_{c}")
-                nc.sync.dma_start(
-                    out=raw[:],
-                    in_=src[K_PASS * c : K_PASS * (c + 1), W * (s % 4) : W * (s % 4) + width].rearrange("(p t) n -> p t n", t=PACK),
-                )
+                rows = src[K_PASS * c : K_PASS * (c + 1), W * (s % 4) : W * (s % 4) + width]
+                if width == N:
+                    nc.sync.dma_start(out=raw[:].rearrange("p t n -> p (t n)"), in_=rows.rearrange("(p t) n -> p (t n)", t=PACK))
+                else:
+                    nc.sync.dma_start(out=raw[:], in_=rows.rearrange("(p t) n -> p t n", t=PACK))
                 for i in range(len(parts)):
-                    raws[f"{s + i}{c}"] = raw[:, :, W * i : W * (i + 1)]
+                    raws[f"{s + i}{c}"] = (raw, W * i)
 
-        ops = {key: operand("op" + key) for key in raws}
+        ops = {key: operand("op" + key) for key in ("a0", "a1", "b")}
+        big = {(t, c): operand(f"big{t}{c}", N) for t in range(2) for c in range(PASSES)}
+        for s in range(8):
+            for c in range(PASSES):
+                ops[f"{s}{c}"] = window(big[(s // 4, c)], W * (s % 4), W * (s % 4 + 1))
         for c in range(PASSES):
             nc.vector.memset(ops[f"a{c}"][2][:].bitcast(I32), 0)
         a4_codes = [sb.tile([P, PACK, TILES, ROWS], I32, name=f"a4_codes{c}", align_bytes=64) for c in range(PASSES)]
@@ -181,26 +189,39 @@ def tile_rows_lora_kernel(tc, x, w, a, bb, out):
             elif name.startswith("lm"):
                 lora_matmuls(int(name[2]))
             elif name.startswith("lc"):
-                g, h = int(name[2]), int(name[3])
-                cols = slice(HALF * h, HALF * (h + 1))
+                g = int(name[2])
+                cols = slice(HALF * int(name[3]), HALF * (int(name[3]) + 1)) if len(name) == 4 else slice(0, N)
                 copy(out=lora_sb[g][:, cols], in_=lora[g][:, cols])
             elif name.startswith("bm"):
                 base_matmuls(int(name[2]), int(name[3]))
             elif name.startswith("ad"):
-                g, h = int(name[2]), int(name[3])
-                cols = slice(HALF * h, HALF * (h + 1))
+                g = int(name[2])
+                h = int(name[3]) if len(name) == 4 else 0
+                cols = slice(HALF * h, HALF * (h + 1)) if len(name) == 4 else slice(0, N)
                 nc.vector.tensor_add(out=result[g][:, cols], in0=base_bank(g, h)[:, cols], in1=lora_sb[g][:, cols])
                 added.add((g, h))
+                if len(name) == 3:
+                    added.add((g, 1))
                 while stores and all(part in added for part in stores[0]):
                     parts = stores.pop(0)
                     g, lo, hi = parts[0][0], HALF * parts[0][1], HALF * (parts[-1][1] + 1)
                     nc.sync.dma_start(out=out[W * g : W * (g + 1), lo:hi], in_=result[g][:, lo:hi])
-            elif name[0] == "c":
-                interleave(copy, ops[name[1:]], raws[name[1:]])
-            elif name[0] == "h":
-                lo = 0 if name[3] == "a" else W // 2
-                interleave(copy, ops[name[1:3]], raws[name[1:3]], lo, lo + W // 2)
-            elif name[0] == "q":
+            elif name == "cb":
+                interleave(copy, ops["b"], raws["b"])
+            elif name in ("qb", "qa0", "qa1"):
                 quantize(ops[name[1:]])
+            elif name[0] in "chq":
+                s, c = int(name[1]), int(name[2])
+                lo, width = 0, W
+                if name[3:4] == "x":
+                    width = W * int(name[4])
+                elif name[3:4] in ("a", "b"):
+                    lo, width = (0 if name[3] == "a" else W // 2), W // 2
+                op = window(big[(s // 4, c)], W * (s % 4) + lo, W * (s % 4) + lo + width)
+                if name[0] == "q":
+                    quantize(op)
+                else:
+                    raw, at = raws[f"{s}{c}"]
+                    interleave(copy, op, raw[:, :, at + lo : at + lo + width], 0, width)
             else:
                 raise ValueError(tok)

@@ -21,8 +21,8 @@ TILES = P // ROWS
 W = 128
 HALF = N // 2
 
-LOADS = "a0 a1 0.0+1.0+2.0+3.0 0.1+1.1 2.1+3.1 b 4.0+5.0+6.0+7.0 4.1+5.1 6.1 7.1"
-ORDER = "Vca0 Vqa0 Vca1 Vra0 Vqa1 Vra1 Vc00x2 Sc20x2 Vq00x2 Vq20x2 Vc01 Sc11 Vq01 Vq11 Pzm0 Pzm1 Vc21 Vh31a Sh31b Vq21 Vq31 Szc0 Pzm2 Vcb Szc1 Pzm3 Vqz0 Vqb Vzc2 Plm0 Vqz1 Szc3 Vqz2 Plm1 Plm2 Vc40 Sc60x2 Vqz3 Plm3 Vc50 Vq40x2 Slc0 Slc1 Vc41 Vc51 Vq41 Vq51 Pbm00 Pbm01 Pbm10 Pbm11 Vq60x2 Sc61 Vh71a Sh71b Vq61 Vq71 Pbm20 Pbm21 Slc2 Slc3 Vad0 Vad1 Pbm30 Pbm31 Vad2 Vad30 Vad31"
+LOADS = "a0 a1 0.0+1.0+2.0+3.0 0.1+1.1+2.1+3.1 4.0+5.0+6.0+7.0 b 4.1+5.1 6.1 7.1"
+ORDER = "Vca0 Vca1 Vqa0 Vqa1 Vra0 Vra1 Pwu:a1:12 Vc00 Sc20 Vc10 Sc30 Vq00 Vq20 Vq10 Vq30 Pwu:30:10 Vc01 Sc11 Vq01 Pzm0 Vc21 Sc31 Vq11 Pzm1 Vq21 Pzm2 Vq31 Pzm3 Szc0 Vc40 Sc60 Vc50 Vq40 Vqz0 Szc1 Vcb Vq50 Pwu:50:4 Vq60 Pwu:60:4 Vqz1 Szc2 Vqb Plm0 Plm1 Vqz2 Plm2 Szc3 Vc41 Sc51 Vqz3 Plm3 Vq41 Pbm00 Pbm01 Sc70 Vc61 Vq51 Pbm10 Pbm11 Vq61 Vq70 Pbm20 Pbm21 Slc00 Slc01 Vh71a Sh71b Vad00 Vad01 Vq71 Slc10 Slc11 Pbm30 Pbm31 Vad10 Vad11 Slc20 Slc21 Vad20 Vad21 Slc30 Slc31 Vad30 Vad31"
 
 
 def tile_rows_lora_kernel(tc, x, w, a, bb, out):
@@ -171,7 +171,7 @@ def tile_rows_lora_kernel(tc, x, w, a, bb, out):
                     )
 
         added = set()
-        stores = [((0, 0), (0, 1)), ((1, 0), (1, 1)), ((2, 0), (2, 1)), ((3, 0),), ((3, 1),)]
+        stores = [((0, 0),), ((0, 1),), ((1, 0), (1, 1)), ((2, 0), (2, 1)), ((3, 0),), ((3, 1),)]
         for tok in ORDER.split():
             copy = {"V": nc.vector.tensor_copy, "S": nc.scalar.copy, "G": gpsimd_copy, "P": None}[tok[0]]
             name = tok[1:]
@@ -181,6 +181,19 @@ def tile_rows_lora_kernel(tc, x, w, a, bb, out):
                 replicate(int(name[2]))
             elif name.startswith("zm"):
                 z_matmuls(int(name[2]))
+            elif name.startswith("wu"):
+                src, count = name.split(":")[1:]
+                bank = whole[0] if src[0] in "4567" else whole[3]
+                for i in range(int(count)):
+                    nc.tensor.matmul_mx(
+                        out=bank[:, :W],
+                        lhsT=a4_codes[0][:, 0].rearrange("p g q -> p (g q)").bitcast(FP8X4),
+                        lhsT_scale=a4_scales[0][:, 0].rearrange("p g q -> p (g q)").bitcast(U8),
+                        rhs=ops[src][1][:].bitcast(FP8X4),
+                        rhs_scale=ops[src][2][:],
+                        start=True,
+                        stop=True,
+                    )
             elif name.startswith("zc"):
                 i = int(name[2])
                 copy(out=z_ops[i][0][:], in_=whole[i][:].rearrange("p (j n) -> p n j", j=PACK))

@@ -20,221 +20,219 @@ ROWS = R // PACK
 TILES = P // ROWS
 W = 128
 HALF = N // 2
+RUN = 4
 
-LOADS = "a0 a1 0.0+1.0+2.0+3.0 0.1+1.1+2.1+3.1 4.0+5.0+6.0+7.0 b 4.1+5.1 6.1 7.1"
-ORDER = "Vca0 Vca1 Vqa0 Vqa1 Vra0 Vra1 Pwu:a1:12 Vc00 Sc20 Vc10 Sc30 Vq00 Vq20 Vq10 Vq30 Pwu:30:10 Vc01 Sc11 Vq01 Pzm0 Vc21 Sc31 Vq11 Pzm1 Vq21 Pzm2 Vq31 Pzm3 Szc0 Vc40 Sc60 Vc50 Vq40 Vqz0 Szc1 Vcb Vq50 Pwu:50:4 Vq60 Pwu:60:4 Vqz1 Szc2 Vqb Plm0 Plm1 Vqz2 Plm2 Szc3 Vc41 Sc51 Vqz3 Plm3 Vq41 Pbm00 Pbm01 Sc70 Vc61 Vq51 Pbm10 Pbm11 Vq61 Vq70 Pbm20 Pbm21 Slc00 Slc01 Vh71a Sh71b Vad00 Vad01 Vq71 Slc10 Slc11 Pbm30 Pbm31 Vad10 Vad11 Slc20 Slc21 Vad20 Vad21 Slc30 Slc31 Vad30 Vad31"
+WARM_A, WARM_X, WARM_W0, WARM_W1 = 14, 9, 6, 2
 
 
 def tile_rows_lora_kernel(tc, x, w, a, bb, out):
     nc = tc.nc
+    on_vector, on_scalar = nc.vector.tensor_copy, nc.scalar.copy
 
     with ExitStack() as ctx:
         sb = ctx.enter_context(tc.tile_pool(name="sb", bufs=1))
         ps = ctx.enter_context(tc.psum_pool(name="ps", bufs=1))
         ctx.enter_context(tc.manual_schedule())
 
-        whole = [ps.tile([P, N], F32, name=f"whole{i}") for i in range(4)]
-        lora = [ps.tile([P, N], F32, name=f"lora{g}") for g in range(TILES)]
+        whole_banks = [ps.tile([P, N], F32, name=f"whole_bank{i}") for i in range(TILES)]
+        row_banks = [ps.tile([P, N], F32, name=f"row_bank{g}") for g in range(TILES)]
 
-        def operand(name, width=W):
-            staged = sb.tile([P, width, PACK], BF16, name=name + "_bf", align_bytes=64)
+        def operand(name, width):
+            staged = sb.tile([P, width, PACK], BF16, name=name + "_staged", align_bytes=64)
             codes = sb.tile([P, width], U32, name=name + "_codes", align_bytes=64)
             scales = sb.tile([P, width], U8, name=name + "_scales", align_bytes=64)
             return staged, codes, scales
 
-        def quantize(op):
+        def chunks(first, count=1):
+            return slice(W * first, W * (first + count))
+
+        def quantize(op, cols):
             staged, codes, scales = op
             nc.vector.quantize_mx(
-                out=codes[:].bitcast(FP8X4),
-                scales=scales[:],
-                in_=staged[:].rearrange("p n t -> p (n t)"),
+                out=codes[:, cols].bitcast(FP8X4),
+                scales=scales[:, cols],
+                in_=staged[:, cols, :].rearrange("p n t -> p (n t)"),
             )
 
-        def window(op, lo, hi):
-            return op[0][:, lo:hi, :], op[1][:, lo:hi], op[2][:, lo:hi]
-
-        def gpsimd_copy(out, in_):
-            nc.gpsimd.tensor_scalar(out=out, in0=in_, scalar1=1.0, scalar2=0.0, op0=mybir.AluOpType.mult, op1=mybir.AluOpType.add)
-
-        def interleave(copy, op, raw, lo=0, hi=W):
+        def interleave(copy, op, cols, raw):
             copy(
-                out=op[0][:, lo:hi, :].rearrange("p (c i) t -> p c t i", i=4),
-                in_=raw[:, :, lo:hi].rearrange("p t (c i) -> p c t i", i=4),
+                out=op[0][:, cols, :].rearrange("p (u i) t -> p u t i", i=RUN),
+                in_=raw.rearrange("p t (u i) -> p u t i", i=RUN),
             )
 
-        warm = sb.tile([P, 8], F32, name="warm")
-        warm2 = sb.tile([P, 8], F32, name="warm2")
-        nc.vector.memset(warm[:], 0.0)
-        nc.scalar.copy(out=warm2[:], in_=warm[:])
+        def multiply(acc, lhs_codes, lhs_scales, rhs_codes, rhs_scales, start, stop):
+            nc.tensor.matmul_mx(
+                out=acc,
+                lhsT=lhs_codes.bitcast(FP8X4),
+                lhsT_scale=lhs_scales,
+                rhs=rhs_codes.bitcast(FP8X4),
+                rhs_scale=rhs_scales,
+                start=start,
+                stop=stop,
+            )
 
-        raws = {}
-        for tok in LOADS.split():
-            if tok[0] == "a":
-                c = int(tok[1])
-                raw = sb.tile([P, PACK, R], F32, name=f"a_raw{c}")
-                nc.sync.dma_start(
-                    out=raw[:].rearrange("p t r -> p (t r)"), in_=a[K_PASS * c : K_PASS * (c + 1), :].rearrange("(p t) r -> p (t r)", t=PACK)
-                )
-                raws[tok] = raw[:]
-            elif tok == "b":
-                raw = sb.tile([P, PACK, W], F32, name="bb_raw")
-                for g in (0, 2, 1, 3):
-                    nc.sync.dma_start(
-                        out=raw[ROWS * g : ROWS * (g + 1)],
-                        in_=bb[:, W * g : W * (g + 1)].rearrange("(p t) m -> p t m", t=PACK),
-                    )
-                raws[tok] = raw[:]
-            else:
-                parts = tok.split("+")
-                s, c = int(parts[0][0]), int(parts[0][2])
-                src = x if s < 4 else w
-                width = W * len(parts)
-                raw = sb.tile([P, PACK, width], F32, name=f"raw{s}_{c}")
-                rows = src[K_PASS * c : K_PASS * (c + 1), W * (s % 4) : W * (s % 4) + width]
-                if width == N:
-                    nc.sync.dma_start(out=raw[:].rearrange("p t n -> p (t n)"), in_=rows.rearrange("(p t) n -> p (t n)", t=PACK))
-                else:
-                    nc.sync.dma_start(out=raw[:], in_=rows.rearrange("(p t) n -> p t n", t=PACK))
-                for i in range(len(parts)):
-                    raws[f"{s + i}{c}"] = (raw, W * i)
+        def load_pass(name, src, c):
+            raw = sb.tile([P, PACK, src.shape[1]], F32, name=name)
+            nc.sync.dma_start(
+                out=raw[:].rearrange("p t n -> p (t n)"),
+                in_=src[K_PASS * c : K_PASS * (c + 1), :].rearrange("(p t) n -> p (t n)", t=PACK),
+            )
+            return raw
 
-        ops = {key: operand("op" + key) for key in ("a0", "a1", "b")}
-        big = {(t, c): operand(f"big{t}{c}", N) for t in range(2) for c in range(PASSES)}
-        for s in range(8):
-            for c in range(PASSES):
-                ops[f"{s}{c}"] = window(big[(s // 4, c)], W * (s % 4), W * (s % 4 + 1))
-        for c in range(PASSES):
-            nc.vector.memset(ops[f"a{c}"][2][:].bitcast(I32), 0)
+        def load_columns(name, src, c, cols):
+            raw = sb.tile([P, PACK, cols.stop - cols.start], F32, name=name)
+            nc.sync.dma_start(
+                out=raw[:], in_=src[K_PASS * c : K_PASS * (c + 1), cols].rearrange("(p t) n -> p t n", t=PACK)
+            )
+            return raw
+
+        a_raw = [load_pass(f"a_raw{c}", a, c) for c in range(PASSES)]
+        x_raw = [load_pass(f"x_raw{c}", x, c) for c in range(PASSES)]
+        w0_raw = load_pass("w0_raw", w, 0)
+        bb_raw = sb.tile([P, PACK, W], F32, name="bb_raw")
+        for g in (0, 2, 1, 3):
+            nc.sync.dma_start(
+                out=bb_raw[ROWS * g : ROWS * (g + 1)], in_=bb[:, chunks(g)].rearrange("(q t) m -> q t m", t=PACK)
+            )
+        w1_raw01 = load_columns("w1_raw01", w, 1, chunks(0, 2))
+        w1_raw2 = load_columns("w1_raw2", w, 1, chunks(2))
+        w1_raw3 = load_columns("w1_raw3", w, 1, chunks(3))
+
+        a_op = [operand(f"a{c}", R) for c in range(PASSES)]
+        x_op = [operand(f"x{c}", N) for c in range(PASSES)]
+        w_op = [operand(f"w{c}", M) for c in range(PASSES)]
+        bb_op = operand("bb", W)
+        z_op = operand("z", N)
         a4_codes = [sb.tile([P, PACK, TILES, ROWS], I32, name=f"a4_codes{c}", align_bytes=64) for c in range(PASSES)]
-        a4_scales = [sb.tile([P, PACK, TILES, ROWS // 4], I32, name=f"a4_scales{c}", align_bytes=64) for c in range(PASSES)]
-        z_ops = [operand(f"z{i}") for i in range(4)]
-        lora_sb = [sb.tile([P, N], F32, name=f"lora_sb{g}") for g in range(TILES)]
+        a4_scales = [
+            sb.tile([P, PACK, TILES, ROWS // 4], I32, name=f"a4_scales{c}", align_bytes=64) for c in range(PASSES)
+        ]
+        branch = [sb.tile([P, N], F32, name=f"branch{g}") for g in range(TILES)]
         result = [sb.tile([P, N], F32, name=f"result{g}") for g in range(TILES)]
 
-        def cast_a(copy, c):
+        def deal_a(copy, c):
             copy(
-                out=ops[f"a{c}"][0][:].rearrange("p (j q) t -> p q j t", j=PACK),
-                in_=raws[f"a{c}"].rearrange("p t (q j) -> p q j t", j=PACK),
+                out=a_op[c][0][:].rearrange("p (j q) t -> p q j t", j=PACK),
+                in_=a_raw[c][:].rearrange("p t (q j) -> p q j t", j=PACK),
             )
 
-        def replicate(c):
-            op = ops[f"a{c}"]
-            nc.vector.tensor_copy(
-                out=a4_codes[c][:],
-                in_=op[1][:].bitcast(I32).rearrange("p (u q) -> p u q", q=ROWS).unsqueeze(2).to_broadcast([P, PACK, TILES, ROWS]),
-            )
-            nc.vector.tensor_copy(
-                out=a4_scales[c][:],
-                in_=op[2][:].bitcast(I32).rearrange("p (u q) -> p u q", q=ROWS // 4).unsqueeze(2).to_broadcast([P, PACK, TILES, ROWS // 4]),
+        def repeat_a(c):
+            for dst, src in ((a4_codes[c], a_op[c][1]), (a4_scales[c], a_op[c][2])):
+                runs = src[:].bitcast(I32).rearrange("p (j q) -> p j q", j=PACK)
+                nc.vector.tensor_copy(out=dst[:], in_=runs.unsqueeze(2).to_broadcast(dst.shape))
+
+        def a4(c, j):
+            return (
+                a4_codes[c][:, j].rearrange("p g q -> p (g q)"),
+                a4_scales[c][:, j].rearrange("p g q -> p (g q)").bitcast(U8),
             )
 
-        def z_matmuls(i):
+        def keep_warm(bank, op, cols, count):
+            for i in range(count):
+                multiply(bank[:, chunks(0)], *a4(1, 0), op[1][:, cols], op[2][:, cols], True, True)
+
+        def z_passes(i):
             for j in range(PACK):
                 for c in range(PASSES):
-                    nc.tensor.matmul_mx(
-                        out=whole[i][:, W * j : W * (j + 1)],
-                        lhsT=a4_codes[c][:, j].rearrange("p g q -> p (g q)").bitcast(FP8X4),
-                        lhsT_scale=a4_scales[c][:, j].rearrange("p g q -> p (g q)").bitcast(U8),
-                        rhs=ops[f"{i}{c}"][1][:].bitcast(FP8X4),
-                        rhs_scale=ops[f"{i}{c}"][2][:],
-                        start=(c == 0),
-                        stop=(c == PASSES - 1),
+                    multiply(
+                        whole_banks[i][:, chunks(j)], *a4(c, j),
+                        x_op[c][1][:, chunks(i)], x_op[c][2][:, chunks(i)], c == 0, c == PASSES - 1,
                     )
 
-        def lora_matmuls(i):
+        def z_out(i):
+            on_scalar(out=z_op[0][:, chunks(i), :], in_=whole_banks[i][:].rearrange("p (j n) -> p n j", j=PACK))
+
+        def branch_passes(i):
             for g in range(TILES):
                 rows = slice(ROWS * g, ROWS * (g + 1))
-                nc.tensor.matmul_mx(
-                    out=lora[g][:, W * i : W * (i + 1)],
-                    lhsT=ops["b"][1][rows, :].bitcast(FP8X4),
-                    lhsT_scale=ops["b"][2][rows, :],
-                    rhs=z_ops[i][1][rows, :].bitcast(FP8X4),
-                    rhs_scale=z_ops[i][2][rows, :],
-                    start=True,
-                    stop=True,
+                multiply(
+                    row_banks[g][:, chunks(i)], bb_op[1][rows, :], bb_op[2][rows, :],
+                    z_op[1][rows, chunks(i)], z_op[2][rows, chunks(i)], True, True,
                 )
 
-        def base_bank(g, h):
-            return whole[0] if (g == 3 and h == 1) else whole[g]
-
-        def base_matmuls(g, h):
-            for i in (2 * h, 2 * h + 1):
+        def base_passes(bank, g, first, count):
+            for i in range(first, first + count):
                 for c in range(PASSES):
-                    nc.tensor.matmul_mx(
-                        out=base_bank(g, h)[:, W * i : W * (i + 1)],
-                        lhsT=ops[f"{4 + g}{c}"][1][:].bitcast(FP8X4),
-                        lhsT_scale=ops[f"{4 + g}{c}"][2][:],
-                        rhs=ops[f"{i}{c}"][1][:].bitcast(FP8X4),
-                        rhs_scale=ops[f"{i}{c}"][2][:],
-                        start=(c == 0),
-                        stop=(c == PASSES - 1),
+                    multiply(
+                        bank[:, chunks(i)], w_op[c][1][:, chunks(g)], w_op[c][2][:, chunks(g)],
+                        x_op[c][1][:, chunks(i)], x_op[c][2][:, chunks(i)], c == 0, c == PASSES - 1,
                     )
 
-        added = set()
-        stores = [((0, 0),), ((0, 1),), ((1, 0), (1, 1)), ((2, 0), (2, 1)), ((3, 0),), ((3, 1),)]
-        for tok in ORDER.split():
-            copy = {"V": nc.vector.tensor_copy, "S": nc.scalar.copy, "G": gpsimd_copy, "P": None}[tok[0]]
-            name = tok[1:]
-            if name.startswith("ca"):
-                cast_a(copy, int(name[2]))
-            elif name.startswith("ra"):
-                replicate(int(name[2]))
-            elif name.startswith("zm"):
-                z_matmuls(int(name[2]))
-            elif name.startswith("wu"):
-                src, count = name.split(":")[1:]
-                bank = whole[0] if src[0] in "4567" else whole[3]
-                for i in range(int(count)):
-                    nc.tensor.matmul_mx(
-                        out=bank[:, :W],
-                        lhsT=a4_codes[0][:, 0].rearrange("p g q -> p (g q)").bitcast(FP8X4),
-                        lhsT_scale=a4_scales[0][:, 0].rearrange("p g q -> p (g q)").bitcast(U8),
-                        rhs=ops[src][1][:].bitcast(FP8X4),
-                        rhs_scale=ops[src][2][:],
-                        start=True,
-                        stop=True,
-                    )
-            elif name.startswith("zc"):
-                i = int(name[2])
-                copy(out=z_ops[i][0][:], in_=whole[i][:].rearrange("p (j n) -> p n j", j=PACK))
-            elif name.startswith("qz"):
-                quantize(z_ops[int(name[2])])
-            elif name.startswith("lm"):
-                lora_matmuls(int(name[2]))
-            elif name.startswith("lc"):
-                g = int(name[2])
-                cols = slice(HALF * int(name[3]), HALF * (int(name[3]) + 1)) if len(name) == 4 else slice(0, N)
-                copy(out=lora_sb[g][:, cols], in_=lora[g][:, cols])
-            elif name.startswith("bm"):
-                base_matmuls(int(name[2]), int(name[3]))
-            elif name.startswith("ad"):
-                g = int(name[2])
-                h = int(name[3]) if len(name) == 4 else 0
-                cols = slice(HALF * h, HALF * (h + 1)) if len(name) == 4 else slice(0, N)
-                nc.vector.tensor_add(out=result[g][:, cols], in0=base_bank(g, h)[:, cols], in1=lora_sb[g][:, cols])
-                added.add((g, h))
-                if len(name) == 3:
-                    added.add((g, 1))
-                while stores and all(part in added for part in stores[0]):
-                    parts = stores.pop(0)
-                    g, lo, hi = parts[0][0], HALF * parts[0][1], HALF * (parts[-1][1] + 1)
-                    nc.sync.dma_start(out=out[W * g : W * (g + 1), lo:hi], in_=result[g][:, lo:hi])
-            elif name == "cb":
-                interleave(copy, ops["b"], raws["b"])
-            elif name in ("qb", "qa0", "qa1"):
-                quantize(ops[name[1:]])
-            elif name[0] in "chq":
-                s, c = int(name[1]), int(name[2])
-                lo, width = 0, W
-                if name[3:4] == "x":
-                    width = W * int(name[4])
-                elif name[3:4] in ("a", "b"):
-                    lo, width = (0 if name[3] == "a" else W // 2), W // 2
-                op = window(big[(s // 4, c)], W * (s % 4) + lo, W * (s % 4) + lo + width)
-                if name[0] == "q":
-                    quantize(op)
-                else:
-                    raw, at = raws[f"{s}{c}"]
-                    interleave(copy, op, raw[:, :, at + lo : at + lo + width], 0, width)
-            else:
-                raise ValueError(tok)
+        def branch_out(g, cols):
+            on_scalar(out=branch[g][:, cols], in_=row_banks[g][:, cols])
+
+        def add_and_store(bank, g, cols):
+            nc.vector.tensor_add(out=result[g][:, cols], in0=bank[:, cols], in1=branch[g][:, cols])
+            nc.sync.dma_start(out=out[chunks(g), cols], in_=result[g][:, cols])
+
+
+        for c in range(PASSES):
+            nc.vector.memset(a_op[c][2][:].bitcast(I32), 0)
+        deal_a(on_scalar, 0)
+        deal_a(on_vector, 1)
+        quantize(a_op[1], chunks(0))
+        repeat_a(1)
+        keep_warm(whole_banks[3], a_op[1], chunks(0), WARM_A)
+        quantize(a_op[0], chunks(0))
+        repeat_a(0)
+
+        interleave(on_vector, x_op[0], chunks(0, 2), x_raw[0][:, :, chunks(0, 2)])
+        interleave(on_scalar, x_op[0], chunks(2), x_raw[0][:, :, chunks(2)])
+        interleave(on_vector, x_op[0], chunks(3), x_raw[0][:, :, chunks(3)])
+        quantize(x_op[0], chunks(0, 2))
+        quantize(x_op[0], chunks(2, 2))
+        keep_warm(whole_banks[3], x_op[0], chunks(2), WARM_X)
+
+        interleave(on_vector, x_op[1], chunks(0), x_raw[1][:, :, chunks(0)])
+        interleave(on_scalar, x_op[1], chunks(1), x_raw[1][:, :, chunks(1)])
+        quantize(x_op[1], chunks(0))
+        z_passes(0)
+        interleave(on_vector, x_op[1], chunks(2), x_raw[1][:, :, chunks(2)])
+        quantize(x_op[1], chunks(1))
+        z_passes(1)
+        interleave(on_scalar, x_op[1], chunks(3), x_raw[1][:, :, chunks(3)])
+        quantize(x_op[1], chunks(2, 2))
+        z_passes(2)
+        z_passes(3)
+
+        for i in range(TILES):
+            z_out(i)
+        interleave(on_vector, w_op[0], chunks(0, 2), w0_raw[:, :, chunks(0, 2)])
+        interleave(on_vector, w_op[0], chunks(2, 2), w0_raw[:, :, chunks(2, 2)])
+        quantize(w_op[0], chunks(0, 2))
+        interleave(on_vector, bb_op, chunks(0), bb_raw[:])
+        quantize(z_op, chunks(0, 2))
+        keep_warm(whole_banks[0], w_op[0], chunks(0), WARM_W0)
+        quantize(bb_op, chunks(0))
+        branch_passes(0)
+        branch_passes(1)
+        quantize(z_op, chunks(2, 2))
+        branch_passes(2)
+        branch_passes(3)
+
+        interleave(on_scalar, w_op[1], chunks(0), w1_raw01[:, :, chunks(0)])
+        interleave(on_scalar, w_op[1], chunks(1), w1_raw01[:, :, chunks(1)])
+        quantize(w_op[0], chunks(2, 2))
+        keep_warm(whole_banks[0], w_op[0], chunks(2), WARM_W1)
+        quantize(w_op[1], chunks(0))
+        base_passes(whole_banks[0], 0, 0, 4)
+        interleave(on_vector, w_op[1], chunks(2), w1_raw2[:])
+        quantize(w_op[1], chunks(1))
+        base_passes(whole_banks[1], 1, 0, 4)
+        interleave(on_vector, w_op[1], slice(3 * W, 3 * W + W // 2), w1_raw3[:, :, : W // 2])
+        quantize(w_op[1], chunks(2))
+        base_passes(whole_banks[2], 2, 0, 4)
+        branch_out(0, slice(0, N))
+        interleave(on_scalar, w_op[1], slice(3 * W + W // 2, M), w1_raw3[:, :, W // 2 :])
+        add_and_store(whole_banks[0], 0, slice(0, N))
+        quantize(w_op[1], chunks(3))
+        base_passes(whole_banks[3], 3, 0, 2)
+        base_passes(whole_banks[0], 3, 2, 2)
+        branch_out(1, slice(0, N))
+        branch_out(2, slice(0, N))
+        branch_out(3, slice(0, HALF))
+        branch_out(3, slice(HALF, N))
+        add_and_store(whole_banks[1], 1, slice(0, N))
+        add_and_store(whole_banks[2], 2, slice(0, N))
+        add_and_store(whole_banks[3], 3, slice(0, HALF))
+        add_and_store(whole_banks[0], 3, slice(HALF, N))

@@ -22,7 +22,7 @@ W = 128
 HALF = N // 2
 RUN = 4
 
-WARM_A, WARM_X, WARM_W0, WARM_W1 = 14, 9, 6, 2
+WARM_A, WARM_X, WARM_W0, WARM_W1 = 12, 9, 6, 2
 
 
 def tile_rows_lora_kernel(tc, x, w, a, bb, out):
@@ -98,38 +98,31 @@ def tile_rows_lora_kernel(tc, x, w, a, bb, out):
         w1_raw2 = load_columns("w1_raw2", w, 1, chunks(2))
         w1_raw3 = load_columns("w1_raw3", w, 1, chunks(3))
 
-        a_op = [operand(f"a{c}", R) for c in range(PASSES)]
+        a_op = operand("a", PASSES * R)
         x_op = [operand(f"x{c}", N) for c in range(PASSES)]
         w_op = [operand(f"w{c}", M) for c in range(PASSES)]
         bb_op = operand("bb", W)
         z_op = operand("z", N)
-        a4_codes = [sb.tile([P, PACK, TILES, ROWS], I32, name=f"a4_codes{c}", align_bytes=64) for c in range(PASSES)]
-        a4_scales = [
-            sb.tile([P, PACK, TILES, ROWS // 4], I32, name=f"a4_scales{c}", align_bytes=64) for c in range(PASSES)
-        ]
+        a4_codes = sb.tile([P, PASSES * PACK, TILES, ROWS], I32, name="a4_codes", align_bytes=64)
+        a4_scales = sb.tile([P, PASSES * PACK, TILES, ROWS // 4], I32, name="a4_scales", align_bytes=64)
         branch = [sb.tile([P, N], F32, name=f"branch{g}") for g in range(TILES)]
         result = [sb.tile([P, N], F32, name=f"result{g}") for g in range(TILES)]
 
         def deal_a(copy, c):
             copy(
-                out=a_op[c][0][:].rearrange("p (j q) t -> p q j t", j=PACK),
+                out=a_op[0][:, chunks(c), :].rearrange("p (j q) t -> p q j t", j=PACK),
                 in_=a_raw[c][:].rearrange("p t (q j) -> p q j t", j=PACK),
             )
 
-        def repeat_a(c):
-            for dst, src in ((a4_codes[c], a_op[c][1]), (a4_scales[c], a_op[c][2])):
-                runs = src[:].bitcast(I32).rearrange("p (j q) -> p j q", j=PACK)
-                nc.vector.tensor_copy(out=dst[:], in_=runs.unsqueeze(2).to_broadcast(dst.shape))
-
         def a4(c, j):
             return (
-                a4_codes[c][:, j].rearrange("p g q -> p (g q)"),
-                a4_scales[c][:, j].rearrange("p g q -> p (g q)").bitcast(U8),
+                a4_codes[:, PACK * c + j].rearrange("p g q -> p (g q)"),
+                a4_scales[:, PACK * c + j].rearrange("p g q -> p (g q)").bitcast(U8),
             )
 
         def keep_warm(bank, op, cols, count):
             for i in range(count):
-                multiply(bank[:, chunks(0)], *a4(1, 0), op[1][:, cols], op[2][:, cols], True, True)
+                multiply(bank[:, chunks(0)], *a4(0, 0), op[1][:, cols], op[2][:, cols], True, True)
 
         def z_passes(i):
             for j in range(PACK):
@@ -166,19 +159,17 @@ def tile_rows_lora_kernel(tc, x, w, a, bb, out):
             nc.sync.dma_start(out=out[chunks(g), cols], in_=result[g][:, cols])
 
 
-        for c in range(PASSES):
-            nc.vector.memset(a_op[c][2][:].bitcast(I32), 0)
-        deal_a(on_scalar, 0)
-        deal_a(on_vector, 1)
-        quantize(a_op[1], chunks(0))
-        repeat_a(1)
-        keep_warm(whole_banks[3], a_op[1], chunks(0), WARM_A)
-        quantize(a_op[0], chunks(0))
-        repeat_a(0)
+        nc.vector.memset(a_op[2][:].bitcast(I32), 0)
+        deal_a(on_vector, 0)
+        deal_a(on_scalar, 1)
+        quantize(a_op, chunks(0, PASSES))
+        for repeated, once in ((a4_codes, a_op[1]), (a4_scales, a_op[2])):
+            runs = once[:].bitcast(I32).rearrange("p (u q) -> p u q", u=PASSES * PACK)
+            on_vector(out=repeated[:], in_=runs.unsqueeze(2).to_broadcast(repeated.shape))
+        keep_warm(whole_banks[3], a_op, chunks(0), WARM_A)
 
         interleave(on_vector, x_op[0], chunks(0, 2), x_raw[0][:, :, chunks(0, 2)])
-        interleave(on_scalar, x_op[0], chunks(2), x_raw[0][:, :, chunks(2)])
-        interleave(on_vector, x_op[0], chunks(3), x_raw[0][:, :, chunks(3)])
+        interleave(on_scalar, x_op[0], chunks(2, 2), x_raw[0][:, :, chunks(2, 2)])
         quantize(x_op[0], chunks(0, 2))
         quantize(x_op[0], chunks(2, 2))
         keep_warm(whole_banks[3], x_op[0], chunks(2), WARM_X)
@@ -197,13 +188,12 @@ def tile_rows_lora_kernel(tc, x, w, a, bb, out):
 
         for i in range(TILES):
             z_out(i)
-        interleave(on_vector, w_op[0], chunks(0, 2), w0_raw[:, :, chunks(0, 2)])
-        interleave(on_vector, w_op[0], chunks(2, 2), w0_raw[:, :, chunks(2, 2)])
-        quantize(w_op[0], chunks(0, 2))
+        interleave(on_vector, w_op[0], chunks(0, 4), w0_raw[:])
         interleave(on_vector, bb_op, chunks(0), bb_raw[:])
+        quantize(w_op[0], chunks(0, 2))
+        quantize(bb_op, chunks(0))
         quantize(z_op, chunks(0, 2))
         keep_warm(whole_banks[0], w_op[0], chunks(0), WARM_W0)
-        quantize(bb_op, chunks(0))
         branch_passes(0)
         branch_passes(1)
         quantize(z_op, chunks(2, 2))

from contextlib import ExitStack

import concourse.mybir as mybir

K, R, M, N = 1024, 128, 512, 512
FLOPS = 2 * K * N * (M + R) + 2 * R * M * N

F32 = mybir.dt.float32
BF16 = mybir.dt.bfloat16
I32 = mybir.dt.int32
U32 = mybir.dt.uint32
U8 = mybir.dt.uint8
FP8X4 = mybir.dt.float8_e4m3fn_x4

P = 128
PACK = 4
K_PASS = P * PACK
PASSES = K // K_PASS
ROWS = R // PACK
TILES = P // ROWS
W = 128
HALF = N // 2
RUN = 4

WARM_A, WARM_X, WARM_W0, WARM_W1 = 12, 9, 6, 2


def tile_rows_lora_kernel(tc, x, w, a, bb, out):
    nc = tc.nc
    on_vector, on_scalar = nc.vector.tensor_copy, nc.scalar.copy

    with ExitStack() as ctx:
        sb = ctx.enter_context(tc.tile_pool(name="sb", bufs=1))
        ps = ctx.enter_context(tc.psum_pool(name="ps", bufs=1))
        ctx.enter_context(tc.manual_schedule())

        whole_banks = [ps.tile([P, N], F32, name=f"whole_bank{i}") for i in range(TILES)]
        row_banks = [ps.tile([P, N], F32, name=f"row_bank{g}") for g in range(TILES)]

        def operand(name, width):
            staged = sb.tile([P, width, PACK], BF16, name=name + "_staged", align_bytes=64)
            codes = sb.tile([P, width], U32, name=name + "_codes", align_bytes=64)
            scales = sb.tile([P, width], U8, name=name + "_scales", align_bytes=64)
            return staged, codes, scales

        def chunks(first, count=1):
            return slice(W * first, W * (first + count))

        def quantize(op, cols):
            staged, codes, scales = op
            nc.vector.quantize_mx(
                out=codes[:, cols].bitcast(FP8X4),
                scales=scales[:, cols],
                in_=staged[:, cols, :].rearrange("p n t -> p (n t)"),
            )

        def interleave(copy, op, cols, raw):
            copy(
                out=op[0][:, cols, :].rearrange("p (u i) t -> p u t i", i=RUN),
                in_=raw.rearrange("p t (u i) -> p u t i", i=RUN),
            )

        def multiply(acc, lhs_codes, lhs_scales, rhs_codes, rhs_scales, start, stop):
            nc.tensor.matmul_mx(
                out=acc,
                lhsT=lhs_codes.bitcast(FP8X4),
                lhsT_scale=lhs_scales,
                rhs=rhs_codes.bitcast(FP8X4),
                rhs_scale=rhs_scales,
                start=start,
                stop=stop,
            )

        def load_pass(name, src, c):
            raw = sb.tile([P, PACK, src.shape[1]], F32, name=name)
            nc.sync.dma_start(
                out=raw[:].rearrange("p t n -> p (t n)"),
                in_=src[K_PASS * c : K_PASS * (c + 1), :].rearrange("(p t) n -> p (t n)", t=PACK),
            )
            return raw

        def load_columns(name, src, c, cols):
            raw = sb.tile([P, PACK, cols.stop - cols.start], F32, name=name)
            nc.sync.dma_start(
                out=raw[:], in_=src[K_PASS * c : K_PASS * (c + 1), cols].rearrange("(p t) n -> p t n", t=PACK)
            )
            return raw

        a_raw = [load_pass(f"a_raw{c}", a, c) for c in range(PASSES)]
        x_raw = [load_pass(f"x_raw{c}", x, c) for c in range(PASSES)]
        w0_raw = load_pass("w0_raw", w, 0)
        bb_raw = sb.tile([P, PACK, W], F32, name="bb_raw")
        for g in (0, 2, 1, 3):
            nc.sync.dma_start(
                out=bb_raw[ROWS * g : ROWS * (g + 1)], in_=bb[:, chunks(g)].rearrange("(q t) m -> q t m", t=PACK)
            )
        w1_raw01 = load_columns("w1_raw01", w, 1, chunks(0, 2))
        w1_raw2 = load_columns("w1_raw2", w, 1, chunks(2))
        w1_raw3 = load_columns("w1_raw3", w, 1, chunks(3))

        a_op = operand("a", PASSES * R)
        x_op = [operand(f"x{c}", N) for c in range(PASSES)]
        w_op = [operand(f"w{c}", M) for c in range(PASSES)]
        bb_op = operand("bb", W)
        z_op = operand("z", N)
        a4_codes = sb.tile([P, PASSES * PACK, TILES, ROWS], I32, name="a4_codes", align_bytes=64)
        a4_scales = sb.tile([P, PASSES * PACK, TILES, ROWS // 4], I32, name="a4_scales", align_bytes=64)
        branch = [sb.tile([P, N], F32, name=f"branch{g}") for g in range(TILES)]
        result = [sb.tile([P, N], F32, name=f"result{g}") for g in range(TILES)]

        def deal_a(copy, c):
            copy(
                out=a_op[0][:, chunks(c), :].rearrange("p (j q) t -> p q j t", j=PACK),
                in_=a_raw[c][:].rearrange("p t (q j) -> p q j t", j=PACK),
            )

        def a4(c, j):
            return (
                a4_codes[:, PACK * c + j].rearrange("p g q -> p (g q)"),
                a4_scales[:, PACK * c + j].rearrange("p g q -> p (g q)").bitcast(U8),
            )

        def keep_warm(bank, op, cols, count):
            for i in range(count):
                multiply(bank[:, chunks(0)], *a4(0, 0), op[1][:, cols], op[2][:, cols], True, True)

        def z_passes(i):
            for j in range(PACK):
                for c in range(PASSES):
                    multiply(
                        whole_banks[i][:, chunks(j)], *a4(c, j),
                        x_op[c][1][:, chunks(i)], x_op[c][2][:, chunks(i)], c == 0, c == PASSES - 1,
                    )

        def z_out(i):
            on_scalar(out=z_op[0][:, chunks(i), :], in_=whole_banks[i][:].rearrange("p (j n) -> p n j", j=PACK))

        def branch_passes(i):
            for g in range(TILES):
                rows = slice(ROWS * g, ROWS * (g + 1))
                multiply(
                    row_banks[g][:, chunks(i)], bb_op[1][rows, :], bb_op[2][rows, :],
                    z_op[1][rows, chunks(i)], z_op[2][rows, chunks(i)], True, True,
                )

        def base_passes(bank, g, first, count):
            for i in range(first, first + count):
                for c in range(PASSES):
                    multiply(
                        bank[:, chunks(i)], w_op[c][1][:, chunks(g)], w_op[c][2][:, chunks(g)],
                        x_op[c][1][:, chunks(i)], x_op[c][2][:, chunks(i)], c == 0, c == PASSES - 1,
                    )

        def branch_out(g, cols):
            on_scalar(out=branch[g][:, cols], in_=row_banks[g][:, cols])

        def add_and_store(bank, g, cols):
            nc.vector.tensor_add(out=result[g][:, cols], in0=bank[:, cols], in1=branch[g][:, cols])
            nc.sync.dma_start(out=out[chunks(g), cols], in_=result[g][:, cols])


        nc.vector.memset(a_op[2][:].bitcast(I32), 0)
        deal_a(on_vector, 0)
        deal_a(on_scalar, 1)
        quantize(a_op, chunks(0, PASSES))
        for repeated, once in ((a4_codes, a_op[1]), (a4_scales, a_op[2])):
            runs = once[:].bitcast(I32).rearrange("p (u q) -> p u q", u=PASSES * PACK)
            on_vector(out=repeated[:], in_=runs.unsqueeze(2).to_broadcast(repeated.shape))
        keep_warm(whole_banks[3], a_op, chunks(0), WARM_A)

        interleave(on_vector, x_op[0], chunks(0, 2), x_raw[0][:, :, chunks(0, 2)])
        interleave(on_scalar, x_op[0], chunks(2, 2), x_raw[0][:, :, chunks(2, 2)])
        quantize(x_op[0], chunks(0, 2))
        quantize(x_op[0], chunks(2, 2))
        keep_warm(whole_banks[3], x_op[0], chunks(2), WARM_X)

        interleave(on_vector, x_op[1], chunks(0), x_raw[1][:, :, chunks(0)])
        interleave(on_scalar, x_op[1], chunks(1), x_raw[1][:, :, chunks(1)])
        quantize(x_op[1], chunks(0))
        z_passes(0)
        interleave(on_vector, x_op[1], chunks(2), x_raw[1][:, :, chunks(2)])
        quantize(x_op[1], chunks(1))
        z_passes(1)
        interleave(on_scalar, x_op[1], chunks(3), x_raw[1][:, :, chunks(3)])
        quantize(x_op[1], chunks(2, 2))
        z_passes(2)
        z_passes(3)

        for i in range(TILES):
            z_out(i)
        interleave(on_vector, w_op[0], chunks(0, 4), w0_raw[:])
        interleave(on_vector, bb_op, chunks(0), bb_raw[:])
        quantize(w_op[0], chunks(0, 2))
        quantize(bb_op, chunks(0))
        quantize(z_op, chunks(0, 2))
        keep_warm(whole_banks[0], w_op[0], chunks(0), WARM_W0)
        branch_passes(0)
        branch_passes(1)
        quantize(z_op, chunks(2, 2))
        branch_passes(2)
        branch_passes(3)

        interleave(on_scalar, w_op[1], chunks(0), w1_raw01[:, :, chunks(0)])
        interleave(on_scalar, w_op[1], chunks(1), w1_raw01[:, :, chunks(1)])
        quantize(w_op[0], chunks(2, 2))
        keep_warm(whole_banks[0], w_op[0], chunks(2), WARM_W1)
        quantize(w_op[1], chunks(0))
        base_passes(whole_banks[0], 0, 0, 4)
        interleave(on_vector, w_op[1], chunks(2), w1_raw2[:])
        quantize(w_op[1], chunks(1))
        base_passes(whole_banks[1], 1, 0, 4)
        interleave(on_vector, w_op[1], slice(3 * W, 3 * W + W // 2), w1_raw3[:, :, : W // 2])
        quantize(w_op[1], chunks(2))
        base_passes(whole_banks[2], 2, 0, 4)
        branch_out(0, slice(0, N))
        interleave(on_scalar, w_op[1], slice(3 * W + W // 2, M), w1_raw3[:, :, W // 2 :])
        add_and_store(whole_banks[0], 0, slice(0, N))
        quantize(w_op[1], chunks(3))
        base_passes(whole_banks[3], 3, 0, 2)
        base_passes(whole_banks[0], 3, 2, 2)
        branch_out(1, slice(0, N))
        branch_out(2, slice(0, N))
        branch_out(3, slice(0, HALF))
        branch_out(3, slice(HALF, N))
        add_and_store(whole_banks[1], 1, slice(0, N))
        add_and_store(whole_banks[2], 2, slice(0, N))
        add_and_store(whole_banks[3], 3, slice(0, HALF))
        add_and_store(whole_banks[0], 3, slice(HALF, N))
